import numpy as np
import ml_dtypes


def mxq(x, axis, fmt="e4m3"):
    dtype, down = {"e4m3": (ml_dtypes.float8_e4m3fn, 7), "e5m2": (ml_dtypes.float8_e5m2, 14)}[fmt]
    v = np.moveaxis(np.asarray(x, np.float32).astype(ml_dtypes.bfloat16).astype(np.float64), axis, -1)
    blocks = v.reshape(v.shape[:-1] + (-1, 32))
    amax = np.abs(blocks).max(-1, keepdims=True)
    byte = np.maximum(np.where(amax > 0, np.frexp(amax)[1] - 1 + 127, 0) - down, 1)
    scale = np.exp2(byte - 127.0)
    codes = (blocks / scale).astype(np.float32).astype(dtype).astype(np.float64)
    return np.moveaxis((codes * scale).reshape(v.shape), -1, axis)


WIDE = False


def mx_kscale(k):
    if not WIDE:
        return np.ones(k)
    levels = np.array([30, -30])
    if k % 512:
        return np.exp2(np.random.permutation(np.resize(levels, k // 32))).repeat(32)
    a = np.empty((k // 512, 16))
    for p in range(k // 512):
        a[p, :8] = np.random.permutation(np.resize(levels, 8))
        for g in range(8):
            far = levels[np.abs(levels - a[p, g]) >= 10]
            a[p, g + 8] = far[np.random.randint(len(far))]
    return np.exp2(a.ravel()).repeat(32)


def f64(x):
    return np.asarray(x).astype(np.float64)


def striped(idx):
    return np.tile(np.asarray(idx).reshape(-1, 16).T, (8, 1)).astype(np.uint16)


def unstriped(offs):
    return offs[:16].T.reshape(-1).astype(np.int64)


E2M1 = np.array([0.0, 0.5, 1.0, 1.5, 2.0, 3.0, 4.0, 6.0, -0.0, -0.5, -1.0, -1.5, -2.0, -3.0, -4.0, -6.0])


def pack_weight(w, fmt):
    k, n = w.shape
    w = f64(np.asarray(w, np.float32).astype(ml_dtypes.bfloat16)).reshape(k // 32, 32, n)
    amax = np.abs(w).max(1)
    if fmt in ("e4m3", "e5m2"):
        byte = np.frexp(amax)[1] - 1 + 127 - (7 if fmt == "e4m3" else 14)
    else:
        mant, ex = np.frexp(amax / 6.0)
        byte = np.where(mant > 0.5, ex, ex - 1) + 127
    byte = np.clip(np.where(amax > 0, byte, 1), 1, 254)
    scaled = (w * np.exp2(127.0 - byte)[:, None, :]).reshape(k, n).astype(np.float32)
    by_word = np.ascontiguousarray(scaled.reshape(k // 512, 128, 4, n).transpose(0, 1, 3, 2))
    if fmt in ("e4m3", "e5m2"):
        words = by_word.astype(ml_dtypes.float8_e4m3fn if fmt == "e4m3" else ml_dtypes.float8_e5m2).view(np.uint8)
    else:
        c = by_word.astype(ml_dtypes.float4_e2m1fn).view(np.uint8) & 0xF
        words = (c[..., 0::2] | (c[..., 1::2] << 4)).reshape(k // 512, 128, 2 * n)
    return np.ascontiguousarray(words), np.ascontiguousarray(byte.astype(np.uint8).reshape(k // 512, 16, n))


def unpack_weight(words, scales, fmt):
    g, _, n = scales.shape
    words = np.ascontiguousarray(words).reshape(g, 128, n, -1)
    if fmt in ("e4m3", "e5m2"):
        vals = words.view(ml_dtypes.float8_e4m3fn if fmt == "e4m3" else ml_dtypes.float8_e5m2).astype(np.float64)
    else:
        nib = np.empty((g, 128, n, 4), np.uint8)
        nib[..., 0::2] = words & 0xF
        nib[..., 1::2] = words >> 4
        vals = E2M1[nib]
    vals = vals * np.repeat(np.exp2(scales.astype(np.float64) - 127.0), 8, axis=1)[..., None]
    return vals.transpose(0, 1, 3, 2).reshape(g * 512, n)


K, T, I, J, N, Z, S, V, E = 512, 1024, 512, 256, 256, 1024, 1024, 1024, 1024


def setup_inputs():
    n = np.random.standard_normal
    idx = np.random.permutation(T)[:I]
    idx2 = np.random.permutation(Z)[:J]
    idx3 = np.random.permutation(V)[:J]
    idx4 = np.random.permutation(S)[:N]
    idx5 = np.random.permutation(E)[:J]
    fk = mx_kscale(K)
    fi = mx_kscale(I)
    ti = np.ones(T)
    ti[idx] = fi
    xkp = pack_weight(n((K, T)) * 0.3 * fk[:, None] * ti, "e5m2")
    xqp = pack_weight(n((K, Z)) * 0.3 / fk[:, None], "e2m1")
    xrp = pack_weight(n((K, V)) * 0.3 / fk[:, None], "e5m2")
    vsp = pack_weight(n((I, S)) / fi[:, None], "e5m2")
    return {
        "xk_words": xkp[0],
        "xk_scales": xkp[1],
        "xq_words": xqp[0],
        "xq_scales": xqp[1],
        "xr_words": xrp[0],
        "xr_scales": xrp[1],
        "vs_words": vsp[0],
        "vs_scales": vsp[1],
        "offs": striped(idx),
        "offs2": striped(idx2),
        "offs3": striped(idx3),
        "offs4": striped(idx4),
        "offs5": striped(idx5),
    }


def reference(xk_words, xk_scales, xq_words, xq_scales, xr_words, xr_scales, vs_words, vs_scales, offs, offs2, offs3, offs4, offs5):
    idx = unstriped(offs)
    idx2 = unstriped(offs2)
    idx3 = unstriped(offs3)
    idx4 = unstriped(offs4)
    idx5 = unstriped(offs5)
    xku = unpack_weight(xk_words, xk_scales, "e5m2")
    xqu = unpack_weight(xq_words, xq_scales, "e2m1")
    xru = unpack_weight(xr_words, xr_scales, "e5m2")
    vsu = unpack_weight(vs_words, vs_scales, "e5m2")
    xkidxg = xku[:, idx]
    xqidx2g = xqu[:, idx2]
    s1 = xkidxg.T @ xqidx2g
    xridx3g = xru[:, idx3]
    s2 = xkidxg.T @ xridx3g
    hid = np.maximum(s1 - s2, 0.0)
    vsidx4g = vsu[:, idx4]
    hidq = mxq(hid, 0, "e4m3")
    p = vsidx4g.T @ hidq
    y = np.zeros((N, E))
    y[:, idx5] = p
    return y

@@ -1,0 +1,153 @@
+from contextlib import ExitStack
+
+import concourse.mybir as mybir
+
+K, T, I, J, N, E = 512, 1024, 512, 256, 256, 1024
+FLOPS = 2 * K * I * J * 2 + 2 * I * N * J
+
+F32 = mybir.dt.float32
+BF16 = mybir.dt.bfloat16
+I32 = mybir.dt.int32
+U32 = mybir.dt.uint32
+U16 = mybir.dt.uint16
+U8 = mybir.dt.uint8
+E4M3 = mybir.dt.float8_e4m3fn_x4
+E5M2 = mybir.dt.float8_e5m2_x4
+E2M1 = mybir.dt.float4_e2m1fn_x4
+ACT = mybir.ActivationFunctionType
+ALU = mybir.AluOpType
+
+P = 128
+PACK = 4
+CHUNK = 128
+CHUNKS = J // CHUNK
+GROUP = 16
+
+
+def tile_list_contest_rivals_direct_scattered_kernel(
+    tc, xk_words, xk_scales, xq_words, xq_scales, xr_words, xr_scales, vs_words, vs_scales,
+    offs, offs2, offs3, offs4, offs5, out,
+):
+    nc = tc.nc
+    with ExitStack() as ctx:
+        sb = ctx.enter_context(tc.tile_pool(name="sb", bufs=1))
+        ps = ctx.enter_context(tc.psum_pool(name="ps", bufs=1))
+
+        def load_list(name, src):
+            tile = sb.tile(list(src.shape), U16, name=name)
+            nc.sync.dma_start(tile[:], src)
+            return tile
+
+        def zeroed_plane(name, eng):
+            tile = sb.tile([P, T], U8, name=name, align_bytes=64)
+            eng.memset(tile[:].bitcast(I32), 0)
+            return tile
+
+        def load_scales(tile, src, queue):
+            for q in range(4):
+                queue.dma_start(tile[32 * q : 32 * q + 4, :].bitcast(I32), src[0, 4 * q : 4 * q + 4, :].bitcast(I32))
+
+        def load_words(name, src_rows, dtype, queue):
+            tile = sb.tile([P, T], dtype, name=name, align_bytes=64)
+            queue.dma_start(tile[:].bitcast(I32), src_rows.bitcast(I32))
+            return tile
+
+        def gather(name, window, offsets, count, dtype):
+            tile = sb.tile([P, count], dtype, name=name, align_bytes=64)
+            nc.vector.tensor_copy(tile[:], window[:].indirect(offsets))
+            return tile
+
+        xk_plane = zeroed_plane("xk_plane", nc.vector)
+        xq_plane = zeroed_plane("xq_plane", nc.vector)
+        xr_plane = zeroed_plane("xr_plane", nc.vector)
+        vs_plane = zeroed_plane("vs_plane", nc.gpsimd)
+
+        key_list = load_list("key_list", offs)
+        load_scales(xk_plane, xk_scales, nc.sync)
+        xk_table = load_words("xk_table", xk_words[0].rearrange("p c r -> p (c r)"), U32, nc.sync)
+        query_list = load_list("query_list", offs2)
+        xq_table = load_words("xq_table", xq_words[0], U16, nc.sync)
+        load_scales(xq_plane, xq_scales, nc.sync)
+        xr_table = load_words("xr_table", xr_words[0].rearrange("p c r -> p (c r)"), U32, nc.sync)
+        rival_list = load_list("rival_list", offs3)
+        load_scales(xr_plane, xr_scales, nc.sync)
+        load_scales(vs_plane, vs_scales, nc.gpsimd)
+        vs_table = load_words("vs_table", vs_words[0].rearrange("p c r -> p (c r)"), U32, nc.sync)
+        entry_list = load_list("entry_list", offs4)
+        place_list = load_list("place_list", offs5)
+
+        pages = []
+        for h in range(N // P):
+            page = sb.tile([P, E], F32, name=f"page{h}")
+            nc.vector.memset(page[:], 0.0)
+            pages.append(page)
+
+        key_scales = sb.tile([P, PACK, P], U8, name="key_scales", align_bytes=64)
+        nc.vector.tensor_copy(key_scales[:].rearrange("p t m -> p m t"), xk_plane[:].indirect(key_list[:]))
+        key_words = sb.tile([P, PACK, P], U32, name="key_words", align_bytes=64)
+        nc.vector.tensor_copy(key_words[:].rearrange("p t m -> p m t"), xk_table[:].indirect(key_list[:]))
+
+        def scores(name, table, plane, lst, c, dtype, mx):
+            cols = lst[:, c * (CHUNK // GROUP) : (c + 1) * (CHUNK // GROUP)]
+            words = gather(f"{name}_words{c}", table, cols, CHUNK, dtype)
+            scales = gather(f"{name}_scales{c}", plane, cols, CHUNK, U8)
+            bank = ps.tile([P, PACK, CHUNK], F32, name=f"{name}_bank{c}")
+            for t in range(PACK):
+                nc.tensor.matmul_mx(
+                    out=bank[:, t, :],
+                    lhsT=key_words[:, t, :].bitcast(E5M2),
+                    lhsT_scale=key_scales[:, t, :],
+                    rhs=words[:].bitcast(mx),
+                    rhs_scale=scales[:],
+                    start=True,
+                    stop=True,
+                )
+            return bank
+
+        s1 = []
+        for c in range(CHUNKS):
+            bank = scores("query", xq_table, xq_plane, query_list, c, U16, E2M1)
+            tile = sb.tile([P, CHUNK, PACK], F32, name=f"s1_{c}")
+            nc.scalar.copy(tile[:], bank[:].rearrange("p t j -> p j t"))
+            s1.append(tile)
+        s2 = [scores("rival", xr_table, xr_plane, rival_list, c, U32, E5M2) for c in range(CHUNKS)]
+
+        store_words = gather("store_words", vs_table, entry_list[:], N, U32)
+
+        hid = []
+        for c in range(CHUNKS):
+            diff = sb.tile([P, CHUNK, PACK], F32, name=f"diff{c}")
+            nc.vector.tensor_tensor(diff[:], s1[c][:], s2[c][:].rearrange("p t j -> p j t"), ALU.subtract)
+            kept = sb.tile([P, CHUNK * PACK], BF16, name=f"kept{c}", align_bytes=64)
+            nc.scalar.activation(kept[:], diff[:].rearrange("p j t -> p (j t)"), ACT.Relu)
+            hid.append(kept)
+
+        store_scales = gather("store_scales", vs_plane, entry_list[:], N, U8)
+
+        hid_words = sb.tile([P, J], U32, name="hid_words", align_bytes=64)
+        hid_scales = sb.tile([P, J], U8, name="hid_scales", align_bytes=64)
+        for c in range(CHUNKS):
+            cols = slice(c * CHUNK, (c + 1) * CHUNK)
+            nc.vector.quantize_mx(out=hid_words[:, cols].bitcast(E4M3), scales=hid_scales[:, cols], in_=hid[c][:])
+
+        for h in range(N // P):
+            rows = slice(h * P, (h + 1) * P)
+            bank = ps.tile([P, J], F32, name=f"p_bank{h}")
+            nc.tensor.matmul_mx(
+                out=bank[:],
+                lhsT=store_words[:, rows].bitcast(E5M2),
+                lhsT_scale=store_scales[:, rows],
+                rhs=hid_words[:].bitcast(E4M3),
+                rhs_scale=hid_scales[:],
+                start=True,
+                stop=True,
+            )
+            prod = sb.tile([P, J], F32, name=f"prod{h}")
+            if h == 0:
+                nc.vector.tensor_copy(prod[:], bank[:])
+                nc.vector.tensor_copy(pages[h][:].indirect(place_list[:]), prod[:])
+                nc.sync.dma_start(out[rows, :], pages[h][:])
+            else:
+                nc.scalar.copy(prod[:], bank[:])
+                nc.scalar.activation(pages[h][:].indirect(place_list[:]), prod[:], ACT.Copy)
+                nc.scalar.dma_start(out[rows, :], pages[h][:])

@@ -60,45 +60,46 @@ def tile_list_contest_rivals_direct_scattered_kernel(
         xk_plane = zeroed_plane("xk_plane", nc.vector)
         xq_plane = zeroed_plane("xq_plane", nc.vector)
         xr_plane = zeroed_plane("xr_plane", nc.vector)
-        vs_plane = zeroed_plane("vs_plane", nc.gpsimd)
+        vs_plane = zeroed_plane("vs_plane", nc.vector)
 
+        query_list = load_list("query_list", offs2)
+        xq_table = load_words("xq_table", xq_words[0], U16, nc.sync)
         key_list = load_list("key_list", offs)
         load_scales(xk_plane, xk_scales, nc.sync)
         xk_table = load_words("xk_table", xk_words[0].rearrange("p c r -> p (c r)"), U32, nc.sync)
-        query_list = load_list("query_list", offs2)
-        xq_table = load_words("xq_table", xq_words[0], U16, nc.sync)
         load_scales(xq_plane, xq_scales, nc.sync)
         xr_table = load_words("xr_table", xr_words[0].rearrange("p c r -> p (c r)"), U32, nc.sync)
         rival_list = load_list("rival_list", offs3)
         load_scales(xr_plane, xr_scales, nc.sync)
-        load_scales(vs_plane, vs_scales, nc.gpsimd)
         vs_table = load_words("vs_table", vs_words[0].rearrange("p c r -> p (c r)"), U32, nc.sync)
         entry_list = load_list("entry_list", offs4)
+        load_scales(vs_plane, vs_scales, nc.sync)
         place_list = load_list("place_list", offs5)
 
         pages = []
         for h in range(N // P):
             page = sb.tile([P, E], F32, name=f"page{h}")
-            nc.vector.memset(page[:], 0.0)
+            (nc.gpsimd if h == 0 else nc.vector).memset(page[:].bitcast(I32), 0)
             pages.append(page)
 
+        def chunk_of(lst, c):
+            return lst[:, c * (CHUNK // GROUP) : (c + 1) * (CHUNK // GROUP)]
+
+        query_words = gather("query_words", xq_table, query_list[:], J, U16)
         key_scales = sb.tile([P, PACK, P], U8, name="key_scales", align_bytes=64)
         nc.vector.tensor_copy(key_scales[:].rearrange("p t m -> p m t"), xk_plane[:].indirect(key_list[:]))
         key_words = sb.tile([P, PACK, P], U32, name="key_words", align_bytes=64)
         nc.vector.tensor_copy(key_words[:].rearrange("p t m -> p m t"), xk_table[:].indirect(key_list[:]))
 
-        def scores(name, table, plane, lst, c, dtype, mx):
-            cols = lst[:, c * (CHUNK // GROUP) : (c + 1) * (CHUNK // GROUP)]
-            words = gather(f"{name}_words{c}", table, cols, CHUNK, dtype)
-            scales = gather(f"{name}_scales{c}", plane, cols, CHUNK, U8)
+        def scores(name, words, scales, c, mx):
             bank = ps.tile([P, PACK, CHUNK], F32, name=f"{name}_bank{c}")
             for t in range(PACK):
                 nc.tensor.matmul_mx(
                     out=bank[:, t, :],
                     lhsT=key_words[:, t, :].bitcast(E5M2),
                     lhsT_scale=key_scales[:, t, :],
-                    rhs=words[:].bitcast(mx),
-                    rhs_scale=scales[:],
+                    rhs=words.bitcast(mx),
+                    rhs_scale=scales,
                     start=True,
                     stop=True,
                 )
@@ -106,48 +107,57 @@ def tile_list_contest_rivals_direct_scattered_kernel(
 
         s1 = []
         for c in range(CHUNKS):
-            bank = scores("query", xq_table, xq_plane, query_list, c, U16, E2M1)
+            scales = gather(f"query_scales{c}", xq_plane, chunk_of(query_list, c), CHUNK, U8)
+            bank = scores("query", query_words[:, c * CHUNK : (c + 1) * CHUNK], scales[:], c, E2M1)
             tile = sb.tile([P, CHUNK, PACK], F32, name=f"s1_{c}")
             nc.scalar.copy(tile[:], bank[:].rearrange("p t j -> p j t"))
             s1.append(tile)
-        s2 = [scores("rival", xr_table, xr_plane, rival_list, c, U32, E5M2) for c in range(CHUNKS)]
+        s2 = []
+        for c in range(CHUNKS):
+            words = gather(f"rival_words{c}", xr_table, chunk_of(rival_list, c), CHUNK, U32)
+            scales = gather(f"rival_scales{c}", xr_plane, chunk_of(rival_list, c), CHUNK, U8)
+            s2.append(scores("rival", words[:], scales[:], c, E5M2))
 
         store_words = gather("store_words", vs_table, entry_list[:], N, U32)
 
         hid = []
+        diff = sb.tile([P, J * PACK], F32, name="diff", tag="vs_table", align_bytes=64)
         for c in range(CHUNKS):
-            diff = sb.tile([P, CHUNK, PACK], F32, name=f"diff{c}")
-            nc.vector.tensor_tensor(diff[:], s1[c][:], s2[c][:].rearrange("p t j -> p j t"), ALU.subtract)
+            part = diff[:, c * CHUNK * PACK : (c + 1) * CHUNK * PACK]
+            nc.vector.tensor_tensor(part.rearrange("p (j t) -> p j t", t=PACK), s1[c][:], s2[c][:].rearrange("p t j -> p j t"), ALU.subtract)
             kept = sb.tile([P, CHUNK * PACK], BF16, name=f"kept{c}", align_bytes=64)
-            nc.scalar.activation(kept[:], diff[:].rearrange("p j t -> p (j t)"), ACT.Relu)
+            nc.scalar.activation(kept[:], part, ACT.Relu)
             hid.append(kept)
 
         store_scales = gather("store_scales", vs_plane, entry_list[:], N, U8)
 
-        hid_words = sb.tile([P, J], U32, name="hid_words", align_bytes=64)
-        hid_scales = sb.tile([P, J], U8, name="hid_scales", align_bytes=64)
+        hid_words = sb.tile([P, J], U32, name="hid_words", tag="vs_plane", align_bytes=64)
+        prods = [sb.tile([P, J], F32, name=f"prod{h}") for h in range(N // P)]
         for c in range(CHUNKS):
             cols = slice(c * CHUNK, (c + 1) * CHUNK)
-            nc.vector.quantize_mx(out=hid_words[:, cols].bitcast(E4M3), scales=hid_scales[:, cols], in_=hid[c][:])
+            hid_scales = sb.tile([P, CHUNK], U8, name=f"hid_scales{c}", align_bytes=64)
+            nc.vector.quantize_mx(out=hid_words[:, cols].bitcast(E4M3), scales=hid_scales[:], in_=hid[c][:])
+            for h in range(N // P):
+                rows = slice(h * P, (h + 1) * P)
+                bank = ps.tile([P, CHUNK], F32, name=f"p_bank{h}_{c}")
+                nc.tensor.matmul_mx(
+                    out=bank[:],
+                    lhsT=store_words[:, rows].bitcast(E5M2),
+                    lhsT_scale=store_scales[:, rows],
+                    rhs=hid_words[:, cols].bitcast(E4M3),
+                    rhs_scale=hid_scales[:],
+                    start=True,
+                    stop=True,
+                )
+                if h == 0:
+                    nc.scalar.copy(prods[h][:, cols], bank[:])
+                else:
+                    nc.vector.tensor_copy(prods[h][:, cols], bank[:])
 
-        for h in range(N // P):
-            rows = slice(h * P, (h + 1) * P)
-            bank = ps.tile([P, J], F32, name=f"p_bank{h}")
-            nc.tensor.matmul_mx(
-                out=bank[:],
-                lhsT=store_words[:, rows].bitcast(E5M2),
-                lhsT_scale=store_scales[:, rows],
-                rhs=hid_words[:].bitcast(E4M3),
-                rhs_scale=hid_scales[:],
-                start=True,
-                stop=True,
-            )
-            prod = sb.tile([P, J], F32, name=f"prod{h}")
-            if h == 0:
-                nc.vector.tensor_copy(prod[:], bank[:])
-                nc.vector.tensor_copy(pages[h][:].indirect(place_list[:]), prod[:])
-                nc.sync.dma_start(out[rows, :], pages[h][:])
-            else:
-                nc.scalar.copy(prod[:], bank[:])
-                nc.scalar.activation(pages[h][:].indirect(place_list[:]), prod[:], ACT.Copy)
-                nc.scalar.dma_start(out[rows, :], pages[h][:])
+        for c in range(CHUNKS):
+            cols = slice(c * CHUNK, (c + 1) * CHUNK)
+            places = chunk_of(place_list, c)
+            nc.scalar.activation(pages[0][:].indirect(places), prods[0][:, cols], ACT.Copy)
+            nc.vector.tensor_copy(pages[1][:].indirect(places), prods[1][:, cols])
+        nc.scalar.dma_start(out[0:P, :], pages[0][:])
+        nc.sync.dma_start(out[P : 2 * P, :], pages[1][:])

@@ -57,7 +57,7 @@ def tile_list_contest_rivals_direct_scattered_kernel(
             nc.vector.tensor_copy(tile[:], window[:].indirect(offsets))
             return tile
 
-        xk_plane = zeroed_plane("xk_plane", nc.vector)
+        xk_plane = zeroed_plane("xk_plane", nc.gpsimd)
         xq_plane = zeroed_plane("xq_plane", nc.vector)
         xr_plane = zeroed_plane("xr_plane", nc.vector)
         vs_plane = zeroed_plane("vs_plane", nc.vector)

@@ -43,9 +43,9 @@ def tile_list_contest_rivals_direct_scattered_kernel(
             eng.memset(tile[:].bitcast(I32), 0)
             return tile
 
-        def load_scales(tile, src, queue):
+        def load_scales(tile, src, queue, last_queue=None):
             for q in range(4):
-                queue.dma_start(tile[32 * q : 32 * q + 4, :].bitcast(I32), src[0, 4 * q : 4 * q + 4, :].bitcast(I32))
+                (last_queue if q == 3 and last_queue is not None else queue).dma_start(tile[32 * q : 32 * q + 4, :].bitcast(I32), src[0, 4 * q : 4 * q + 4, :].bitcast(I32))
 
         def load_words(name, src_rows, dtype, queue):
             tile = sb.tile([P, T], dtype, name=name, align_bytes=64)
@@ -57,7 +57,7 @@ def tile_list_contest_rivals_direct_scattered_kernel(
             nc.vector.tensor_copy(tile[:], window[:].indirect(offsets))
             return tile
 
-        xk_plane = zeroed_plane("xk_plane", nc.gpsimd)
+        xk_plane = zeroed_plane("xk_plane", nc.vector)
         xq_plane = zeroed_plane("xq_plane", nc.vector)
         xr_plane = zeroed_plane("xr_plane", nc.vector)
         vs_plane = zeroed_plane("vs_plane", nc.vector)
@@ -68,18 +68,18 @@ def tile_list_contest_rivals_direct_scattered_kernel(
         load_scales(xk_plane, xk_scales, nc.sync)
         xk_table = load_words("xk_table", xk_words[0].rearrange("p c r -> p (c r)"), U32, nc.sync)
         load_scales(xq_plane, xq_scales, nc.sync)
-        xr_table = load_words("xr_table", xr_words[0].rearrange("p c r -> p (c r)"), U32, nc.sync)
         rival_list = load_list("rival_list", offs3)
-        load_scales(xr_plane, xr_scales, nc.sync)
-        vs_table = load_words("vs_table", vs_words[0].rearrange("p c r -> p (c r)"), U32, nc.sync)
         entry_list = load_list("entry_list", offs4)
-        load_scales(vs_plane, vs_scales, nc.sync)
+        xr_table = load_words("xr_table", xr_words[0].rearrange("p c r -> p (c r)"), U32, nc.sync)
+        load_scales(xr_plane, xr_scales, nc.sync)
+        load_scales(vs_plane, vs_scales, nc.sync, last_queue=nc.gpsimd)
+        vs_table = load_words("vs_table", vs_words[0].rearrange("p c r -> p (c r)"), U32, nc.sync)
         place_list = load_list("place_list", offs5)
 
         pages = []
         for h in range(N // P):
             page = sb.tile([P, E], F32, name=f"page{h}")
-            (nc.gpsimd if h == 0 else nc.vector).memset(page[:].bitcast(I32), 0)
+            nc.vector.memset(page[:].bitcast(I32), 0)
             pages.append(page)
 
         def chunk_of(lst, c):
@@ -109,19 +109,19 @@ def tile_list_contest_rivals_direct_scattered_kernel(
         for c in range(CHUNKS):
             scales = gather(f"query_scales{c}", xq_plane, chunk_of(query_list, c), CHUNK, U8)
             bank = scores("query", query_words[:, c * CHUNK : (c + 1) * CHUNK], scales[:], c, E2M1)
-            tile = sb.tile([P, CHUNK, PACK], F32, name=f"s1_{c}")
+            tile = sb.tile([P, CHUNK, PACK], F32, name=f"s1_{c}", align_bytes=64)
             nc.scalar.copy(tile[:], bank[:].rearrange("p t j -> p j t"))
             s1.append(tile)
+        rival_words = gather("rival_words", xr_table, rival_list[:], J, U32)
         s2 = []
         for c in range(CHUNKS):
-            words = gather(f"rival_words{c}", xr_table, chunk_of(rival_list, c), CHUNK, U32)
             scales = gather(f"rival_scales{c}", xr_plane, chunk_of(rival_list, c), CHUNK, U8)
-            s2.append(scores("rival", words[:], scales[:], c, E5M2))
+            s2.append(scores("rival", rival_words[:, c * CHUNK : (c + 1) * CHUNK], scales[:], c, E5M2))
 
-        store_words = gather("store_words", vs_table, entry_list[:], N, U32)
+        store_scales = gather("store_scales", vs_plane, entry_list[:], N, U8)
 
         hid = []
-        diff = sb.tile([P, J * PACK], F32, name="diff", tag="vs_table", align_bytes=64)
+        diff = sb.tile([P, J * PACK], F32, name="diff", tag="vs_plane", align_bytes=64)
         for c in range(CHUNKS):
             part = diff[:, c * CHUNK * PACK : (c + 1) * CHUNK * PACK]
             nc.vector.tensor_tensor(part.rearrange("p (j t) -> p j t", t=PACK), s1[c][:], s2[c][:].rearrange("p t j -> p j t"), ALU.subtract)
@@ -129,35 +129,38 @@ def tile_list_contest_rivals_direct_scattered_kernel(
             nc.scalar.activation(kept[:], part, ACT.Relu)
             hid.append(kept)
 
-        store_scales = gather("store_scales", vs_plane, entry_list[:], N, U8)
-
-        hid_words = sb.tile([P, J], U32, name="hid_words", tag="vs_plane", align_bytes=64)
-        prods = [sb.tile([P, J], F32, name=f"prod{h}") for h in range(N // P)]
+        hid_words = sb.tile([P, J], U32, name="hid_words", align_bytes=64)
+        hid_scales = sb.tile([P, J], U8, name="hid_scales", align_bytes=64)
+        store_words = []
         for c in range(CHUNKS):
             cols = slice(c * CHUNK, (c + 1) * CHUNK)
-            hid_scales = sb.tile([P, CHUNK], U8, name=f"hid_scales{c}", align_bytes=64)
-            nc.vector.quantize_mx(out=hid_words[:, cols].bitcast(E4M3), scales=hid_scales[:], in_=hid[c][:])
-            for h in range(N // P):
-                rows = slice(h * P, (h + 1) * P)
-                bank = ps.tile([P, CHUNK], F32, name=f"p_bank{h}_{c}")
-                nc.tensor.matmul_mx(
-                    out=bank[:],
-                    lhsT=store_words[:, rows].bitcast(E5M2),
-                    lhsT_scale=store_scales[:, rows],
-                    rhs=hid_words[:, cols].bitcast(E4M3),
-                    rhs_scale=hid_scales[:],
-                    start=True,
-                    stop=True,
-                )
-                if h == 0:
-                    nc.scalar.copy(prods[h][:, cols], bank[:])
-                else:
-                    nc.vector.tensor_copy(prods[h][:, cols], bank[:])
+            tile = sb.tile([P, P], U32, name=f"store_words{c}", tag=("s1_1", "kept0")[c], align_bytes=64)
+            nc.vector.tensor_copy(tile[:], vs_table[:].indirect(chunk_of(entry_list, c)))
+            store_words.append(tile)
+            nc.vector.quantize_mx(out=hid_words[:, cols].bitcast(E4M3), scales=hid_scales[:, cols], in_=hid[c][:])
 
-        for c in range(CHUNKS):
-            cols = slice(c * CHUNK, (c + 1) * CHUNK)
-            places = chunk_of(place_list, c)
-            nc.scalar.activation(pages[0][:].indirect(places), prods[0][:, cols], ACT.Copy)
-            nc.vector.tensor_copy(pages[1][:].indirect(places), prods[1][:, cols])
+        def product(name, h, cols):
+            bank = ps.tile([P, cols.stop - cols.start], F32, name=name)
+            nc.tensor.matmul_mx(
+                out=bank[:],
+                lhsT=store_words[h][:].bitcast(E5M2),
+                lhsT_scale=store_scales[:, h * P : (h + 1) * P],
+                rhs=hid_words[:, cols].bitcast(E4M3),
+                rhs_scale=hid_scales[:, cols],
+                start=True,
+                stop=True,
+            )
+            return bank
+
+        first, second = slice(0, CHUNK), slice(CHUNK, J)
+        upper = sb.tile([P, J], F32, name="upper")
+        lower = sb.tile([P, J], F32, name="lower")
+        nc.scalar.copy(upper[:, first], product("upper_first", 0, first)[:])
+        nc.scalar.activation(pages[0][:].indirect(chunk_of(place_list, 0)), upper[:, first], ACT.Copy)
+        nc.vector.tensor_copy(lower[:, first], product("lower_first", 1, first)[:])
+        nc.vector.tensor_copy(upper[:, second], product("upper_second", 0, second)[:])
+        nc.scalar.activation(pages[0][:].indirect(chunk_of(place_list, 1)), upper[:, second], ACT.Copy)
         nc.scalar.dma_start(out[0:P, :], pages[0][:])
+        nc.vector.tensor_copy(lower[:, second], product("lower_second", 1, second)[:])
+        nc.vector.tensor_copy(pages[1][:].indirect(place_list[:]), lower[:])
         nc.sync.dma_start(out[P : 2 * P, :], pages[1][:])

from contextlib import ExitStack

import concourse.mybir as mybir

K, T, I, J, N, E = 512, 1024, 512, 256, 256, 1024
FLOPS = 2 * K * I * J * 2 + 2 * I * N * J

F32 = mybir.dt.float32
BF16 = mybir.dt.bfloat16
I32 = mybir.dt.int32
U32 = mybir.dt.uint32
U16 = mybir.dt.uint16
U8 = mybir.dt.uint8
E4M3 = mybir.dt.float8_e4m3fn_x4
E5M2 = mybir.dt.float8_e5m2_x4
E2M1 = mybir.dt.float4_e2m1fn_x4
ACT = mybir.ActivationFunctionType
ALU = mybir.AluOpType

P = 128
PACK = 4
CHUNK = 128
CHUNKS = J // CHUNK
GROUP = 16


def tile_list_contest_rivals_direct_scattered_kernel(
    tc, xk_words, xk_scales, xq_words, xq_scales, xr_words, xr_scales, vs_words, vs_scales,
    offs, offs2, offs3, offs4, offs5, out,
):
    nc = tc.nc
    with ExitStack() as ctx:
        sb = ctx.enter_context(tc.tile_pool(name="sb", bufs=1))
        ps = ctx.enter_context(tc.psum_pool(name="ps", bufs=1))

        def load_list(name, src):
            tile = sb.tile(list(src.shape), U16, name=name)
            nc.sync.dma_start(tile[:], src)
            return tile

        def zeroed_plane(name, eng):
            tile = sb.tile([P, T], U8, name=name, align_bytes=64)
            eng.memset(tile[:].bitcast(I32), 0)
            return tile

        def load_scales(tile, src, queue, last_queue=None):
            for q in range(4):
                (last_queue if q == 3 and last_queue is not None else queue).dma_start(tile[32 * q : 32 * q + 4, :].bitcast(I32), src[0, 4 * q : 4 * q + 4, :].bitcast(I32))

        def load_words(name, src_rows, dtype, queue):
            tile = sb.tile([P, T], dtype, name=name, align_bytes=64)
            queue.dma_start(tile[:].bitcast(I32), src_rows.bitcast(I32))
            return tile

        def gather(name, window, offsets, count, dtype):
            tile = sb.tile([P, count], dtype, name=name, align_bytes=64)
            nc.vector.tensor_copy(tile[:], window[:].indirect(offsets))
            return tile

        xk_plane = zeroed_plane("xk_plane", nc.vector)
        xq_plane = zeroed_plane("xq_plane", nc.vector)
        xr_plane = zeroed_plane("xr_plane", nc.vector)
        vs_plane = zeroed_plane("vs_plane", nc.vector)

        query_list = load_list("query_list", offs2)
        xq_table = load_words("xq_table", xq_words[0], U16, nc.sync)
        key_list = load_list("key_list", offs)
        load_scales(xk_plane, xk_scales, nc.sync)
        xk_table = load_words("xk_table", xk_words[0].rearrange("p c r -> p (c r)"), U32, nc.sync)
        load_scales(xq_plane, xq_scales, nc.sync)
        rival_list = load_list("rival_list", offs3)
        entry_list = load_list("entry_list", offs4)
        xr_table = load_words("xr_table", xr_words[0].rearrange("p c r -> p (c r)"), U32, nc.sync)
        load_scales(xr_plane, xr_scales, nc.sync)
        load_scales(vs_plane, vs_scales, nc.sync, last_queue=nc.gpsimd)
        vs_table = load_words("vs_table", vs_words[0].rearrange("p c r -> p (c r)"), U32, nc.sync)
        place_list = load_list("place_list", offs5)

        pages = []
        for h in range(N // P):
            page = sb.tile([P, E], F32, name=f"page{h}")
            nc.vector.memset(page[:].bitcast(I32), 0)
            pages.append(page)

        def chunk_of(lst, c):
            return lst[:, c * (CHUNK // GROUP) : (c + 1) * (CHUNK // GROUP)]

        query_words = gather("query_words", xq_table, query_list[:], J, U16)
        key_scales = sb.tile([P, PACK, P], U8, name="key_scales", align_bytes=64)
        nc.vector.tensor_copy(key_scales[:].rearrange("p t m -> p m t"), xk_plane[:].indirect(key_list[:]))
        key_words = sb.tile([P, PACK, P], U32, name="key_words", align_bytes=64)
        nc.vector.tensor_copy(key_words[:].rearrange("p t m -> p m t"), xk_table[:].indirect(key_list[:]))

        def scores(name, words, scales, c, mx):
            bank = ps.tile([P, PACK, CHUNK], F32, name=f"{name}_bank{c}")
            for t in range(PACK):
                nc.tensor.matmul_mx(
                    out=bank[:, t, :],
                    lhsT=key_words[:, t, :].bitcast(E5M2),
                    lhsT_scale=key_scales[:, t, :],
                    rhs=words.bitcast(mx),
                    rhs_scale=scales,
                    start=True,
                    stop=True,
                )
            return bank

        s1 = []
        for c in range(CHUNKS):
            scales = gather(f"query_scales{c}", xq_plane, chunk_of(query_list, c), CHUNK, U8)
            bank = scores("query", query_words[:, c * CHUNK : (c + 1) * CHUNK], scales[:], c, E2M1)
            tile = sb.tile([P, CHUNK, PACK], F32, name=f"s1_{c}", align_bytes=64)
            nc.scalar.copy(tile[:], bank[:].rearrange("p t j -> p j t"))
            s1.append(tile)
        rival_words = gather("rival_words", xr_table, rival_list[:], J, U32)
        s2 = []
        for c in range(CHUNKS):
            scales = gather(f"rival_scales{c}", xr_plane, chunk_of(rival_list, c), CHUNK, U8)
            s2.append(scores("rival", rival_words[:, c * CHUNK : (c + 1) * CHUNK], scales[:], c, E5M2))

        store_scales = gather("store_scales", vs_plane, entry_list[:], N, U8)

        hid = []
        diff = sb.tile([P, J * PACK], F32, name="diff", tag="vs_plane", align_bytes=64)
        for c in range(CHUNKS):
            part = diff[:, c * CHUNK * PACK : (c + 1) * CHUNK * PACK]
            nc.vector.tensor_tensor(part.rearrange("p (j t) -> p j t", t=PACK), s1[c][:], s2[c][:].rearrange("p t j -> p j t"), ALU.subtract)
            kept = sb.tile([P, CHUNK * PACK], BF16, name=f"kept{c}", align_bytes=64)
            nc.scalar.activation(kept[:], part, ACT.Relu)
            hid.append(kept)

        hid_words = sb.tile([P, J], U32, name="hid_words", align_bytes=64)
        hid_scales = sb.tile([P, J], U8, name="hid_scales", align_bytes=64)
        store_words = []
        for c in range(CHUNKS):
            cols = slice(c * CHUNK, (c + 1) * CHUNK)
            tile = sb.tile([P, P], U32, name=f"store_words{c}", tag=("s1_1", "kept0")[c], align_bytes=64)
            nc.vector.tensor_copy(tile[:], vs_table[:].indirect(chunk_of(entry_list, c)))
            store_words.append(tile)
            nc.vector.quantize_mx(out=hid_words[:, cols].bitcast(E4M3), scales=hid_scales[:, cols], in_=hid[c][:])

        def product(name, h, cols):
            bank = ps.tile([P, cols.stop - cols.start], F32, name=name)
            nc.tensor.matmul_mx(
                out=bank[:],
                lhsT=store_words[h][:].bitcast(E5M2),
                lhsT_scale=store_scales[:, h * P : (h + 1) * P],
                rhs=hid_words[:, cols].bitcast(E4M3),
                rhs_scale=hid_scales[:, cols],
                start=True,
                stop=True,
            )
            return bank

        first, second = slice(0, CHUNK), slice(CHUNK, J)
        upper = sb.tile([P, J], F32, name="upper")
        lower = sb.tile([P, J], F32, name="lower")
        nc.scalar.copy(upper[:, first], product("upper_first", 0, first)[:])
        nc.scalar.activation(pages[0][:].indirect(chunk_of(place_list, 0)), upper[:, first], ACT.Copy)
        nc.vector.tensor_copy(lower[:, first], product("lower_first", 1, first)[:])
        nc.vector.tensor_copy(upper[:, second], product("upper_second", 0, second)[:])
        nc.scalar.activation(pages[0][:].indirect(chunk_of(place_list, 1)), upper[:, second], ACT.Copy)
        nc.scalar.dma_start(out[0:P, :], pages[0][:])
        nc.vector.tensor_copy(lower[:, second], product("lower_second", 1, second)[:])
        nc.vector.tensor_copy(pages[1][:].indirect(place_list[:]), lower[:])
        nc.sync.dma_start(out[P : 2 * P, :], pages[1][:])
